import numpy as np
import ml_dtypes


def mxq(x, axis, fmt="e4m3"):
    dtype, down = {"e4m3": (ml_dtypes.float8_e4m3fn, 7), "e5m2": (ml_dtypes.float8_e5m2, 14)}[fmt]
    v = np.moveaxis(np.asarray(x, np.float32).astype(ml_dtypes.bfloat16).astype(np.float64), axis, -1)
    blocks = v.reshape(v.shape[:-1] + (-1, 32))
    amax = np.abs(blocks).max(-1, keepdims=True)
    byte = np.maximum(np.where(amax > 0, np.frexp(amax)[1] - 1 + 127, 0) - down, 1)
    scale = np.exp2(byte - 127.0)
    codes = (blocks / scale).astype(np.float32).astype(dtype).astype(np.float64)
    return np.moveaxis((codes * scale).reshape(v.shape), -1, axis)


WIDE = False


def mx_kscale(k):
    if not WIDE:
        return np.ones(k)
    levels = np.array([10, -10, 5, -5, 0])
    if k % 512:
        return np.exp2(np.random.permutation(np.resize(levels, k // 32))).repeat(32)
    a = np.empty((k // 512, 16))
    for p in range(k // 512):
        a[p, :8] = np.random.permutation(np.resize(levels, 8))
        for g in range(8):
            far = levels[np.abs(levels - a[p, g]) >= 10]
            a[p, g + 8] = far[np.random.randint(len(far))]
    return np.exp2(a.ravel()).repeat(32)


def f64(x):
    return np.asarray(x).astype(np.float64)


def striped(idx):
    return np.tile(idx.reshape(-1, 16).T, (8, 1)).astype(np.uint16)


def unstriped(offs):
    return offs[:16].T.reshape(-1).astype(np.int64)


E2M1 = np.array([0.0, 0.5, 1.0, 1.5, 2.0, 3.0, 4.0, 6.0, -0.0, -0.5, -1.0, -1.5, -2.0, -3.0, -4.0, -6.0])


def pack_weight(w, fmt):
    k, n = w.shape
    w = f64(np.asarray(w, np.float32).astype(ml_dtypes.bfloat16)).reshape(k // 32, 32, n)
    amax = np.abs(w).max(1)
    if fmt == "e4m3":
        byte = np.frexp(amax)[1] - 1 + 127 - 7
    else:
        mant, ex = np.frexp(amax / 6.0)
        byte = np.where(mant > 0.5, ex, ex - 1) + 127
    byte = np.clip(np.where(amax > 0, byte, 1), 1, 254)
    scaled = (w * np.exp2(127.0 - byte)[:, None, :]).reshape(k, n).astype(np.float32)
    by_word = np.ascontiguousarray(scaled.reshape(k // 512, 128, 4, n).transpose(0, 1, 3, 2))
    if fmt == "e4m3":
        words = by_word.astype(ml_dtypes.float8_e4m3fn).view(np.uint8)
    else:
        c = by_word.astype(ml_dtypes.float4_e2m1fn).view(np.uint8) & 0xF
        words = (c[..., 0::2] | (c[..., 1::2] << 4)).reshape(k // 512, 128, 2 * n)
    return np.ascontiguousarray(words), np.ascontiguousarray(byte.astype(np.uint8).reshape(k // 512, 16, n))


def unpack_weight(words, scales, fmt):
    g, _, n = scales.shape
    words = np.ascontiguousarray(words).reshape(g, 128, n, -1)
    if fmt == "e4m3":
        vals = words.view(ml_dtypes.float8_e4m3fn).astype(np.float64)
    else:
        nib = np.empty((g, 128, n, 4), np.uint8)
        nib[..., 0::2] = words & 0xF
        nib[..., 1::2] = words >> 4
        vals = E2M1[nib]
    vals = vals * np.repeat(np.exp2(scales.astype(np.float64) - 127.0), 8, axis=1)[..., None]
    return vals.transpose(0, 1, 3, 2).reshape(g * 512, n)


def gelu(v):
    return 0.5 * v * (1.0 + np.tanh(np.sqrt(2.0 / np.pi) * (v + 0.044715 * v**3)))


K, K1, H, T, S, S2, T3, P = 1024, 512, 1024, 4096, 1024, 1024, 2048, 512

def setup_inputs():
    n = np.random.standard_normal
    s = mx_kscale(K)[:, None]
    u = mx_kscale(H)[:, None]
    tab_words, tab_scales = pack_weight(n((K, T)) * s, "e4m3")
    tab2_words, tab2_scales = pack_weight(n((H, T3)) / np.sqrt(H) / u, "e4m3")
    w1 = (n((K1, H)) / np.sqrt(K) / s[:K1]).astype(np.float32)
    w4_words, w4_scales = pack_weight(n((K - K1, H)) / np.sqrt(K) / s[K1:], "e2m1")
    return {
        "tab_words": tab_words, "tab_scales": tab_scales,
        "offs": striped(np.random.permutation(T)[:S]),
        "tab2_words": tab2_words, "tab2_scales": tab2_scales,
        "offs2": striped(np.random.permutation(T3)[:S2]),
        "pos1": striped(np.random.permutation(S)[:P]),
        "pos2": striped(np.random.permutation(S)[:P]),
        "w1": w1, "w4_words": w4_words, "w4_scales": w4_scales,
        "place": np.random.uniform(0.6, 2.4, S).astype(np.float32),
        "gain": (np.random.uniform(0.7, 1.5, H) * u[:, 0]).astype(np.float32),
        "mood": (6.0 * n((S2, P))).astype(np.float32),
        "cust": np.random.uniform(0.4, 1.4, S2).astype(np.float32),
    }

def reference(tab_words, tab_scales, offs, tab2_words, tab2_scales, offs2, pos1, pos2,
              w1, w4_words, w4_scales, place, gain, mood, cust):
    v = unpack_weight(tab_words, tab_scales, "e4m3")[:, unstriped(offs)]
    v2 = unpack_weight(tab2_words, tab2_scales, "e4m3")[:, unstriped(offs2)]
    w1q = mxq(f64(w1), 0, "e4m3")
    w4 = unpack_weight(w4_words, w4_scales, "e2m1")
    f = w1q.T @ v[:K1] + w4.T @ v[K1:]
    h = f64(gain)[:, None] * np.tanh(f64(place)[None, :] * f)
    hq = mxq(h, 0, "e4m3")
    e = v2.T @ hq
    top = e.max(axis=1)
    a = np.exp(e[:, unstriped(pos1)] - top[:, None])
    c = f64(cust)[:, None] * e[:, unstriped(pos2)]
    return np.maximum(f64(mood) * a, c)

@@ -1,0 +1,240 @@
+from contextlib import ExitStack
+
+import concourse.mybir as mybir
+from concourse.masks import make_identity
+
+K, K1, H, T, S, S2, T3, NP = 1024, 512, 1024, 4096, 1024, 1024, 2048, 512
+FLOPS = 2 * K * H * S + 2 * H * S * S2
+
+F32 = mybir.dt.float32
+BF16 = mybir.dt.bfloat16
+I32 = mybir.dt.int32
+U32 = mybir.dt.uint32
+U16 = mybir.dt.uint16
+U8 = mybir.dt.uint8
+E4M3 = mybir.dt.float8_e4m3fn_x4
+E2M1 = mybir.dt.float4_e2m1fn_x4
+ACT = mybir.ActivationFunctionType
+ALU = mybir.AluOpType
+
+P = 128
+PACK = 4
+BANK = 512
+TILES = S // P
+ON_SCALAR = (4, 5, 6)
+
+
+def tile_list_cellar_bottle_scores_kernel(
+    tc, tab_words, tab_scales, offs, tab2_words, tab2_scales, offs2, pos1, pos2,
+    w1, w4_words, w4_scales, place, gain, mood, cust, out,
+):
+    nc = tc.nc
+    with ExitStack() as ctx:
+        keep = ctx.enter_context(tc.tile_pool(name="keep", bufs=1))
+        ring = ctx.enter_context(tc.tile_pool(name="ring", bufs=3))
+        shared = ctx.enter_context(tc.tile_pool(name="shared", bufs=1))
+        psum = ctx.enter_context(tc.psum_pool(name="psum", bufs=1))
+
+        def held(shape, dtype, name):
+            return keep.tile(shape, dtype, name=name, align_bytes=64)
+
+        def placed(shape, dtype, name, offset):
+            return shared.tile(shape, dtype, name=name, align_bytes=64, offset=offset)
+
+        def words_of(dram):
+            return dram.rearrange("p t i -> p (t i)").bitcast(I32)
+
+        idx = held([P, S // 16], U16, "idx")
+        idx2 = held([P, S2 // 16], U16, "idx2")
+        p1 = held([P, NP // 16], U16, "p1")
+        p2 = held([P, NP // 16], U16, "p2")
+        tab_w = [held([P, T], I32, "tab_w0"), placed([P, T], I32, "tab_w1", T)]
+        tab_s = placed([P, T], U8, "tab_s", 0)
+        tab2_w = [held([P, T3], I32, "tab2_w%d" % a) for a in range(2)]
+        tab2_s = held([P, T3], U8, "tab2_s")
+        w1_raw = [held([P, PACK, BANK], F32, "w1_raw%d" % b) for b in range(2)]
+        w4_w = held([P, 2 * H], U8, "w4_w")
+        w4_s = held([P, H], U8, "w4_s")
+        gain_sb = held([P, 2, PACK], F32, "gain_sb")
+        rows = held([P, P], F32, "rows")
+        cols = held([P, 2 * TILES], F32, "cols")
+        ident = held([P, P], F32, "ident")
+        mood_sb = [held([P, TILES // 2, NP], F32, "mood%d" % g) for g in range(2)]
+
+        nc.vector.memset(rows[:], 0.0)
+        nc.vector.memset(tab_s[:].bitcast(I32), 0)
+        nc.vector.memset(w4_s[:].bitcast(I32), 0)
+        nc.vector.memset(tab2_s[:].bitcast(I32), 0)
+
+        w1_rows = w1.rearrange("(p i) r -> p i r", i=PACK)
+        nc.sync.dma_start(idx[:], offs)
+        nc.sync.dma_start(gain_sb[:], gain.rearrange("(b p i) -> p b i", b=2, i=PACK))
+        nc.sync.dma_start(rows[0:TILES, :], place.rearrange("(t p) -> t p", p=P))
+        nc.sync.dma_start(rows[TILES:2 * TILES, :], cust.rearrange("(t p) -> t p", p=P))
+        nc.sync.dma_start(tab_w[0][:], words_of(tab_words[0]))
+        nc.sync.dma_start(w1_raw[0][:], w1_rows[:, :, 0:BANK])
+        nc.sync.dma_start(w4_w[:].bitcast(I32), w4_words[0].bitcast(I32))
+        nc.sync.dma_start(tab_w[1][:], words_of(tab_words[1]))
+        for r in range(4):
+            nc.sync.dma_start(w4_s[r:P:32, :].bitcast(I32), w4_scales[0, r:16:4, :].bitcast(I32))
+        nc.sync.dma_start(w1_raw[1][:], w1_rows[:, :, BANK:H])
+        nc.sync.dma_start(idx2[:], offs2)
+        for q in range(4):
+            nc.sync.dma_start(tab2_s[32 * q:32 * q + 8, :].bitcast(I32),
+                              tab2_scales[:, 4 * q:4 * q + 4, :].bitcast(I32))
+        for a in range(2):
+            nc.sync.dma_start(tab2_w[a][:], words_of(tab2_words[a]))
+        nc.sync.dma_start(p1[:], pos1)
+        nc.sync.dma_start(p2[:], pos2)
+        mood_rows = mood.rearrange("(t p) n -> p t n", p=P)
+        for g in range(2):
+            nc.sync.dma_start(mood_sb[g][:], mood_rows[:, g * 4:(g + 1) * 4, :])
+
+        for a in range(2):
+            for r in range(4):
+                nc.gpsimd.dma_start(tab_s[4 * (1 - a) + r:P:32, :].bitcast(I32),
+                                    tab_scales[a, r:16:4, :].bitcast(I32))
+        make_identity(nc, ident[:])
+
+        v_w = [held([P, S], U32, "v_w0"), placed([P, S], U32, "v_w1", 0)]
+        v_s = held([P, S], U8, "v_s")
+        v2_w = [placed([P, S2], U32, "v2_w%d" % a, (1 + a) * T) for a in range(2)]
+        v2_s = placed([P, S2], U8, "v2_s", 3 * T)
+        w1_bf = [held([P, BANK, PACK], BF16, "w1_bf0"), placed([P, BANK, PACK], BF16, "w1_bf1", 4 * T)]
+        w1_w = [held([P, BANK], U32, "w1_w%d" % b) for b in range(2)]
+        w1_s = [held([P, BANK], U8, "w1_s%d" % b) for b in range(2)]
+        h_bf = [[held([P, BANK, PACK], BF16, "h_bf%d%d" % (b, g)) for g in range(2)] for b in range(2)]
+        h_w = [[held([P, BANK], U32, "h_w%d%d" % (b, g)) for g in range(2)] for b in range(2)]
+        h_s = [[held([P, BANK], U8, "h_s%d%d" % (b, g)) for g in range(2)] for b in range(2)]
+        e_sb = [held([P, S], F32, "e%d" % t) for t in range(TILES)]
+        half_top = [held([P, 1], F32, "half_top%d" % t) for t in range(TILES)]
+        top = [held([P, 1], F32, "top%d" % t) for t in range(TILES)]
+        neg_top = [held([P, 1], F32, "neg_top%d" % t) for t in range(TILES)]
+
+        def gather_words(dst, table, lst, c0, c1):
+            nc.vector.tensor_copy(dst[:, c0:c1], table[:].bitcast(U32).indirect(lst[:, c0 // 16:c1 // 16]))
+
+        def round_w1(b):
+            nc.scalar.copy(w1_bf[b][:].rearrange("p (c j) i -> p c i j", j=4),
+                           w1_raw[b][:].rearrange("p i (c j) -> p c i j", j=4))
+
+        def quantize(words, scales, values):
+            nc.vector.quantize_mx(out=words[:].bitcast(E4M3), scales=scales[:],
+                                  in_=values[:].rearrange("p c i -> p (c i)"))
+
+        gather_words(v_w[0], tab_w[0], idx, 0, S)
+        round_w1(0)
+        nc.vector.tensor_copy(v_s[:], tab_s[:].indirect(idx[:]))
+        quantize(w1_w[0], w1_s[0], w1_bf[0])
+
+        turned = psum.tile([P, PACK, P], F32, name="turned", tag="turned", bufs=3)
+        nc.tensor.transpose(turned[:, 0, :], rows[:], ident[:])
+        nc.scalar.copy(cols[:], turned[:, 0, 0:2 * TILES])
+
+        for c0 in range(0, S, 256):
+            gather_words(v_w[1], tab_w[1], idx, c0, c0 + 256)
+
+        def features(b, jt):
+            jc = slice(jt * P, (jt + 1) * P)
+            f = psum.tile([P, BANK], F32, name="f", tag="f", bufs=3)
+            nc.tensor.matmul_mx(out=f[:], lhsT=v_w[0][:, jc].bitcast(E4M3), lhsT_scale=v_s[4:P, jc],
+                                rhs=w1_w[b][:].bitcast(E4M3), rhs_scale=w1_s[b][:], start=True, stop=False)
+            nc.tensor.matmul_mx(out=f[:], lhsT=v_w[1][:, jc].bitcast(E4M3), lhsT_scale=v_s[:, jc],
+                                rhs=w4_w[:, 2 * b * BANK:2 * (b + 1) * BANK].bitcast(E2M1),
+                                rhs_scale=w4_s[:, b * BANK:(b + 1) * BANK], start=False, stop=True)
+            th = ring.tile([P, PACK, P], F32, name="th", tag="th", bufs=4)
+            nc.scalar.activation(th[:], f[:].rearrange("p (q i) -> p i q", i=PACK), ACT.Tanh,
+                                 scale=cols[:, jt:jt + 1])
+            return th
+
+        def turn_on_vector(b, jt0, ths):
+            for jt, th in enumerate(ths, jt0):
+                tb = psum.tile([P, PACK, P], F32, name="turned", tag="turned", bufs=3)
+                for i in range(PACK):
+                    nc.tensor.transpose(tb[:, i, :], th[:, i, :], ident[:])
+                j0 = (jt % 4) * P
+                nc.vector.tensor_tensor(h_bf[b][jt // 4][:, j0:j0 + P, :], tb[:].rearrange("p i j -> p j i"),
+                                        gain_sb[:, b:b + 1, :].to_broadcast([P, P, PACK]), ALU.mult)
+
+        def turn_on_scalar(b, jt0, ths):
+            planes = ring.tile([P, PACK, 2 * P], BF16, name="planes", bufs=2)
+            for i0 in range(0, PACK, 2):
+                tb = psum.tile([P, 2, 2 * P], F32, name="turned", tag="turned", bufs=3)
+                for i in range(i0, i0 + 2):
+                    for u, th in enumerate(ths):
+                        nc.tensor.transpose(tb[:, i - i0, u * P:(u + 1) * P], th[:, i, :], ident[:])
+                for i in range(i0, i0 + 2):
+                    nc.scalar.activation(planes[:, i, :], tb[:, i - i0, :], ACT.Copy, scale=gain_sb[:, b, i:i + 1])
+            j0 = (jt0 % 4) * P
+            nc.scalar.copy(h_bf[b][jt0 // 4][:, j0:j0 + 2 * P, :].rearrange("p (c j) i -> p c i j", j=4),
+                           planes[:].rearrange("p i (c j) -> p c i j", j=4))
+
+        def turn(n, b, jt0, ths):
+            (turn_on_scalar if n in ON_SCALAR else turn_on_vector)(b, jt0, ths)
+            if jt0 % 4 == 2:
+                quantize(h_w[b][jt0 // 4], h_s[b][jt0 // 4], h_bf[b][jt0 // 4])
+
+        def scores(t, g):
+            mc = slice(t * P, (t + 1) * P)
+            acc = psum.tile([P, BANK], F32, name="acc", tag="acc", bufs=2)
+            for b in range(2):
+                nc.tensor.matmul_mx(out=acc[:], lhsT=v2_w[b][:, mc].bitcast(E4M3), lhsT_scale=v2_s[4 * b:P, mc],
+                                    rhs=h_w[b][g][:].bitcast(E4M3), rhs_scale=h_s[b][g][:],
+                                    start=(b == 0), stop=(b == 1))
+            nc.vector.tensor_scalar(e_sb[t][:, g * BANK:(g + 1) * BANK], acc[:], 1.0,
+                                    half_top[t][:] if g == 1 else None, ALU.mult, ALU.max,
+                                    accum_out=(top if g == 1 else half_top)[t][:])
+
+        pairs = [(b, jt0) for g in range(2) for b in range(2) for jt0 in (4 * g, 4 * g + 2)]
+        waiting = None
+        for n, (b, jt0) in enumerate(pairs):
+            made = (n, b, jt0, [features(b, jt) for jt in (jt0, jt0 + 1)])
+            if waiting:
+                turn(*waiting)
+            waiting = made
+            if n == 0:
+                round_w1(1)
+            if n == 1:
+                quantize(w1_w[1], w1_s[1], w1_bf[1])
+                nc.vector.tensor_copy(v2_s[:], tab2_s[:].indirect(idx2[:]))
+            if n in (2, 3):
+                for a in range(2):
+                    gather_words(v2_w[a], tab2_w[a], idx2, (n - 2) * BANK, (n - 1) * BANK)
+            if n >= 5:
+                for t in range(2 * (n - 5), 2 * (n - 4)):
+                    scores(t, 0)
+        turn(*waiting)
+        for t in range(6, TILES):
+            scores(t, 0)
+
+        looked, picked, weighed = {}, {}, {}
+
+        def look(t):
+            nc.scalar.mul(neg_top[t][:], top[t][:], -1.0)
+            looked[t] = ring.tile([P, NP], F32, name="looked")
+            nc.scalar.activation(looked[t][:], e_sb[t][:].indirect(p1[:]), ACT.Exp, bias=neg_top[t][:])
+
+        def pick(t):
+            picked[t] = ring.tile([P, NP], F32, name="picked")
+            nc.vector.tensor_copy(picked[t][:], e_sb[t][:].indirect(p2[:]))
+
+        def weigh(t):
+            weighed[t] = ring.tile([P, NP], F32, name="weighed")
+            nc.vector.tensor_tensor(weighed[t][:], looked[t][:], mood_sb[t // 4][:, t % 4, :], ALU.mult)
+
+        def finish(t):
+            res = ring.tile([P, NP], F32, name="res")
+            nc.vector.scalar_tensor_tensor(res[:], picked[t][:], cols[:, TILES + t:TILES + t + 1],
+                                           weighed[t][:], ALU.mult, ALU.max)
+            nc.sync.dma_start(out[t * P:(t + 1) * P, :], res[:])
+
+        for t in range(TILES + 1):
+            if t < TILES:
+                scores(t, 1)
+                look(t)
+            if t > 0:
+                weigh(t - 1)
+            if t < TILES:
+                pick(t)
+            if t > 0:
+                finish(t - 1)

@@ -48,7 +48,7 @@ def tile_list_cellar_bottle_scores_kernel(
         idx2 = held([P, S2 // 16], U16, "idx2")
         p1 = held([P, NP // 16], U16, "p1")
         p2 = held([P, NP // 16], U16, "p2")
-        tab_w = [held([P, T], I32, "tab_w0"), placed([P, T], I32, "tab_w1", T)]
+        tab_w = [held([P, T], I32, "tab_w%d" % a) for a in range(2)]
         tab_s = placed([P, T], U8, "tab_s", 0)
         tab2_w = [held([P, T3], I32, "tab2_w%d" % a) for a in range(2)]
         tab2_s = held([P, T3], U8, "tab2_s")
@@ -98,12 +98,13 @@ def tile_list_cellar_bottle_scores_kernel(
 
         v_w = [held([P, S], U32, "v_w0"), placed([P, S], U32, "v_w1", 0)]
         v_s = held([P, S], U8, "v_s")
-        v2_w = [placed([P, S2], U32, "v2_w%d" % a, (1 + a) * T) for a in range(2)]
-        v2_s = placed([P, S2], U8, "v2_s", 3 * T)
-        w1_bf = [held([P, BANK, PACK], BF16, "w1_bf0"), placed([P, BANK, PACK], BF16, "w1_bf1", 4 * T)]
+        v2_w = [placed([P, S2], U32, "v2_w0", 3 * T), placed([P, S2], U32, "v2_w1", T)]
+        v2_s = placed([P, S2], U8, "v2_s", 2 * T)
+        w1_bf = [held([P, BANK, PACK], BF16, "w1_bf0"), placed([P, BANK, PACK], BF16, "w1_bf1", T)]
         w1_w = [held([P, BANK], U32, "w1_w%d" % b) for b in range(2)]
         w1_s = [held([P, BANK], U8, "w1_s%d" % b) for b in range(2)]
-        h_bf = [[held([P, BANK, PACK], BF16, "h_bf%d%d" % (b, g)) for g in range(2)] for b in range(2)]
+        h_bf = [[placed([P, BANK, PACK], BF16, "h_bf%d%d" % (b, g), (3 + 2 * b + g) * T) for g in range(2)]
+                for b in range(2)]
         h_w = [[held([P, BANK], U32, "h_w%d%d" % (b, g)) for g in range(2)] for b in range(2)]
         h_s = [[held([P, BANK], U8, "h_s%d%d" % (b, g)) for g in range(2)] for b in range(2)]
         e_sb = [held([P, S], F32, "e%d" % t) for t in range(TILES)]
@@ -134,7 +135,7 @@ def tile_list_cellar_bottle_scores_kernel(
         for c0 in range(0, S, 256):
             gather_words(v_w[1], tab_w[1], idx, c0, c0 + 256)
 
-        def features(b, jt):
+        def features(u, b, jt):
             jc = slice(jt * P, (jt + 1) * P)
             f = psum.tile([P, BANK], F32, name="f", tag="f", bufs=3)
             nc.tensor.matmul_mx(out=f[:], lhsT=v_w[0][:, jc].bitcast(E4M3), lhsT_scale=v_s[4:P, jc],
@@ -142,37 +143,47 @@ def tile_list_cellar_bottle_scores_kernel(
             nc.tensor.matmul_mx(out=f[:], lhsT=v_w[1][:, jc].bitcast(E4M3), lhsT_scale=v_s[:, jc],
                                 rhs=w4_w[:, 2 * b * BANK:2 * (b + 1) * BANK].bitcast(E2M1),
                                 rhs_scale=w4_s[:, b * BANK:(b + 1) * BANK], start=False, stop=True)
-            th = ring.tile([P, PACK, P], F32, name="th", tag="th", bufs=4)
+            if u < 3:
+                th = placed([P, PACK, P], F32, "th%d" % u, T + u * T // 2)
+            else:
+                th = ring.tile([P, PACK, P], F32, name="th", tag="th", bufs=6)
             nc.scalar.activation(th[:], f[:].rearrange("p (q i) -> p i q", i=PACK), ACT.Tanh,
                                  scale=cols[:, jt:jt + 1])
             return th
 
-        def turn_on_vector(b, jt0, ths):
-            for jt, th in enumerate(ths, jt0):
-                tb = psum.tile([P, PACK, P], F32, name="turned", tag="turned", bufs=3)
-                for i in range(PACK):
-                    nc.tensor.transpose(tb[:, i, :], th[:, i, :], ident[:])
-                j0 = (jt % 4) * P
-                nc.vector.tensor_tensor(h_bf[b][jt // 4][:, j0:j0 + P, :], tb[:].rearrange("p i j -> p j i"),
-                                        gain_sb[:, b:b + 1, :].to_broadcast([P, P, PACK]), ALU.mult)
+        def turn_on_vector(b, jt, th):
+            tb = psum.tile([P, PACK, P], F32, name="turned", tag="turned", bufs=3)
+            for i in range(PACK):
+                nc.tensor.transpose(tb[:, i, :], th[:, i, :], ident[:])
+            j0 = (jt % 4) * P
+            nc.vector.tensor_tensor(h_bf[b][jt // 4][:, j0:j0 + P, :], tb[:].rearrange("p i j -> p j i"),
+                                    gain_sb[:, b:b + 1, :].to_broadcast([P, P, PACK]), ALU.mult)
 
-        def turn_on_scalar(b, jt0, ths):
-            planes = ring.tile([P, PACK, 2 * P], BF16, name="planes", bufs=2)
-            for i0 in range(0, PACK, 2):
-                tb = psum.tile([P, 2, 2 * P], F32, name="turned", tag="turned", bufs=3)
-                for i in range(i0, i0 + 2):
-                    for u, th in enumerate(ths):
-                        nc.tensor.transpose(tb[:, i - i0, u * P:(u + 1) * P], th[:, i, :], ident[:])
-                for i in range(i0, i0 + 2):
-                    nc.scalar.activation(planes[:, i, :], tb[:, i - i0, :], ACT.Copy, scale=gain_sb[:, b, i:i + 1])
-            j0 = (jt0 % 4) * P
-            nc.scalar.copy(h_bf[b][jt0 // 4][:, j0:j0 + 2 * P, :].rearrange("p (c j) i -> p c i j", j=4),
-                           planes[:].rearrange("p i (c j) -> p c i j", j=4))
+        def turn_on_scalar(b, i0, pair, planes):
+            tb = psum.tile([P, 2, 2 * P], F32, name="turned", tag="turned", bufs=3)
+            for i in range(i0, i0 + 2):
+                for k, th in enumerate(pair):
+                    nc.tensor.transpose(tb[:, i - i0, k * P:(k + 1) * P], th[:, i, :], ident[:])
+            for i in range(i0, i0 + 2):
+                nc.scalar.activation(planes[:, i, :], tb[:, i - i0, :], ACT.Copy, scale=gain_sb[:, b, i:i + 1])
 
-        def turn(n, b, jt0, ths):
-            (turn_on_scalar if n in ON_SCALAR else turn_on_vector)(b, jt0, ths)
-            if jt0 % 4 == 2:
-                quantize(h_w[b][jt0 // 4], h_s[b][jt0 // 4], h_bf[b][jt0 // 4])
+        planes_of = {}
+
+        def turn(u):
+            b, jt = units[u]
+            n, second = divmod(u, 2)
+            if n in ON_SCALAR:
+                if not second:
+                    planes_of[n] = ring.tile([P, PACK, 2 * P], BF16, name="planes", bufs=2)
+                turn_on_scalar(b, 2 * second, tanhs[2 * n:2 * n + 2], planes_of[n])
+                if second:
+                    j0 = ((jt - 1) % 4) * P
+                    nc.scalar.copy(h_bf[b][jt // 4][:, j0:j0 + 2 * P, :].rearrange("p (c j) i -> p c i j", j=4),
+                                   planes_of[n][:].rearrange("p i (c j) -> p c i j", j=4))
+            else:
+                turn_on_vector(b, jt, tanhs[u])
+            if jt % 4 == 3:
+                quantize(h_w[b][jt // 4], h_s[b][jt // 4], h_bf[b][jt // 4])
 
         def scores(t, g):
             mc = slice(t * P, (t + 1) * P)
@@ -185,27 +196,23 @@ def tile_list_cellar_bottle_scores_kernel(
                                     half_top[t][:] if g == 1 else None, ALU.mult, ALU.max,
                                     accum_out=(top if g == 1 else half_top)[t][:])
 
-        pairs = [(b, jt0) for g in range(2) for b in range(2) for jt0 in (4 * g, 4 * g + 2)]
-        waiting = None
-        for n, (b, jt0) in enumerate(pairs):
-            made = (n, b, jt0, [features(b, jt) for jt in (jt0, jt0 + 1)])
-            if waiting:
-                turn(*waiting)
-            waiting = made
-            if n == 0:
+        units = [(b, jt) for g in range(2) for b in range(2) for jt in range(4 * g, 4 * g + 4)]
+        tanhs = []
+        for u in range(len(units) + 2):
+            if u < len(units):
+                tanhs.append(features(u, *units[u]))
+            if u >= 2:
+                turn(u - 2)
+            if u == 3:
                 round_w1(1)
-            if n == 1:
                 quantize(w1_w[1], w1_s[1], w1_bf[1])
+            if u == 4:
                 nc.vector.tensor_copy(v2_s[:], tab2_s[:].indirect(idx2[:]))
-            if n in (2, 3):
-                for a in range(2):
-                    gather_words(v2_w[a], tab2_w[a], idx2, (n - 2) * BANK, (n - 1) * BANK)
-            if n >= 5:
-                for t in range(2 * (n - 5), 2 * (n - 4)):
-                    scores(t, 0)
-        turn(*waiting)
-        for t in range(6, TILES):
-            scores(t, 0)
+            if u in (5, 6, 7, 8):
+                a, half = divmod(u - 5, 2)
+                gather_words(v2_w[a], tab2_w[a], idx2, half * BANK, (half + 1) * BANK)
+            if u >= 10:
+                scores(u - 10, 0)
 
         looked, picked, weighed = {}, {}, {}
 

@@ -21,7 +21,7 @@ P = 128
 PACK = 4
 BANK = 512
 TILES = S // P
-ON_SCALAR = (4, 5, 6)
+ON_SCALAR = (3, 4, 5, 6)
 
 
 def tile_list_cellar_bottle_scores_kernel(
@@ -48,7 +48,7 @@ def tile_list_cellar_bottle_scores_kernel(
         idx2 = held([P, S2 // 16], U16, "idx2")
         p1 = held([P, NP // 16], U16, "p1")
         p2 = held([P, NP // 16], U16, "p2")
-        tab_w = [held([P, T], I32, "tab_w%d" % a) for a in range(2)]
+        tab_w = [placed([P, T], I32, "tab_w0", 8 * T), held([P, T], I32, "tab_w1")]
         tab_s = placed([P, T], U8, "tab_s", 0)
         tab2_w = [held([P, T3], I32, "tab2_w%d" % a) for a in range(2)]
         tab2_s = held([P, T3], U8, "tab2_s")
@@ -56,51 +56,60 @@ def tile_list_cellar_bottle_scores_kernel(
         w4_w = held([P, 2 * H], U8, "w4_w")
         w4_s = held([P, H], U8, "w4_s")
         gain_sb = held([P, 2, PACK], F32, "gain_sb")
-        rows = held([P, P], F32, "rows")
-        cols = held([P, 2 * TILES], F32, "cols")
+        rows = [held([P, P], F32, "rows%d" % k) for k in range(2)]
+        cols = [held([P, TILES], F32, "cols%d" % k) for k in range(2)]
         ident = held([P, P], F32, "ident")
         mood_sb = [held([P, TILES // 2, NP], F32, "mood%d" % g) for g in range(2)]
 
-        nc.vector.memset(rows[:], 0.0)
-        nc.vector.memset(tab_s[:].bitcast(I32), 0)
+        nc.gpsimd.memset(tab_s[:].bitcast(I32), 0)
         nc.vector.memset(w4_s[:].bitcast(I32), 0)
         nc.vector.memset(tab2_s[:].bitcast(I32), 0)
+        for tile in rows:
+            nc.vector.memset(tile[:], 0.0)
+        make_identity(nc, ident[:])
+
+        def load_words(tile, dram, pieces):
+            width = tile.shape[1] // pieces
+            for c0 in range(0, tile.shape[1], width):
+                nc.sync.dma_start(tile[:, c0:c0 + width], words_of(dram)[:, c0:c0 + width])
+
+        def load_tab_scales(n):
+            a, r = divmod(n, 4)
+            nc.sync.dma_start(tab_s[4 * (1 - a) + r:P:32, :].bitcast(I32), tab_scales[a, r:16:4, :].bitcast(I32))
 
         w1_rows = w1.rearrange("(p i) r -> p i r", i=PACK)
+        load_words(tab_w[0], tab_words[0], 2)
         nc.sync.dma_start(idx[:], offs)
-        nc.sync.dma_start(gain_sb[:], gain.rearrange("(b p i) -> p b i", b=2, i=PACK))
-        nc.sync.dma_start(rows[0:TILES, :], place.rearrange("(t p) -> t p", p=P))
-        nc.sync.dma_start(rows[TILES:2 * TILES, :], cust.rearrange("(t p) -> t p", p=P))
-        nc.sync.dma_start(tab_w[0][:], words_of(tab_words[0]))
+        for n in range(5):
+            load_tab_scales(n)
         nc.sync.dma_start(w1_raw[0][:], w1_rows[:, :, 0:BANK])
+        for n in range(5, 8):
+            load_tab_scales(n)
+        load_words(tab_w[1], tab_words[1], 2)
         nc.sync.dma_start(w4_w[:].bitcast(I32), w4_words[0].bitcast(I32))
-        nc.sync.dma_start(tab_w[1][:], words_of(tab_words[1]))
         for r in range(4):
             nc.sync.dma_start(w4_s[r:P:32, :].bitcast(I32), w4_scales[0, r:16:4, :].bitcast(I32))
+        nc.sync.dma_start(rows[0][0:TILES, :], place.rearrange("(t p) -> t p", p=P))
         nc.sync.dma_start(w1_raw[1][:], w1_rows[:, :, BANK:H])
+        nc.sync.dma_start(gain_sb[:], gain.rearrange("(b p i) -> p b i", b=2, i=PACK))
         nc.sync.dma_start(idx2[:], offs2)
         for q in range(4):
             nc.sync.dma_start(tab2_s[32 * q:32 * q + 8, :].bitcast(I32),
                               tab2_scales[:, 4 * q:4 * q + 4, :].bitcast(I32))
         for a in range(2):
-            nc.sync.dma_start(tab2_w[a][:], words_of(tab2_words[a]))
+            load_words(tab2_w[a], tab2_words[a], 1)
+        nc.sync.dma_start(rows[1][0:TILES, :], cust.rearrange("(t p) -> t p", p=P))
         nc.sync.dma_start(p1[:], pos1)
         nc.sync.dma_start(p2[:], pos2)
         mood_rows = mood.rearrange("(t p) n -> p t n", p=P)
         for g in range(2):
             nc.sync.dma_start(mood_sb[g][:], mood_rows[:, g * 4:(g + 1) * 4, :])
 
-        for a in range(2):
-            for r in range(4):
-                nc.gpsimd.dma_start(tab_s[4 * (1 - a) + r:P:32, :].bitcast(I32),
-                                    tab_scales[a, r:16:4, :].bitcast(I32))
-        make_identity(nc, ident[:])
-
         v_w = [held([P, S], U32, "v_w0"), placed([P, S], U32, "v_w1", 0)]
-        v_s = held([P, S], U8, "v_s")
-        v2_w = [placed([P, S2], U32, "v2_w0", 3 * T), placed([P, S2], U32, "v2_w1", T)]
+        v_s = placed([P, S], U8, "v_s", 8 * T)
+        v2_w = [placed([P, S2], U32, "v2_w0", 3 * T), placed([P, S2], U32, "v2_w1", 7 * T)]
         v2_s = placed([P, S2], U8, "v2_s", 2 * T)
-        w1_bf = [held([P, BANK, PACK], BF16, "w1_bf0"), placed([P, BANK, PACK], BF16, "w1_bf1", T)]
+        w1_bf = [held([P, BANK, PACK], BF16, "w1_bf0"), placed([P, BANK, PACK], BF16, "w1_bf1", 7 * T)]
         w1_w = [held([P, BANK], U32, "w1_w%d" % b) for b in range(2)]
         w1_s = [held([P, BANK], U8, "w1_s%d" % b) for b in range(2)]
         h_bf = [[placed([P, BANK, PACK], BF16, "h_bf%d%d" % (b, g), (3 + 2 * b + g) * T) for g in range(2)]
@@ -116,8 +125,12 @@ def tile_list_cellar_bottle_scores_kernel(
             nc.vector.tensor_copy(dst[:, c0:c1], table[:].bitcast(U32).indirect(lst[:, c0 // 16:c1 // 16]))
 
         def round_w1(b):
-            nc.scalar.copy(w1_bf[b][:].rearrange("p (c j) i -> p c i j", j=4),
-                           w1_raw[b][:].rearrange("p i (c j) -> p c i j", j=4))
+            if b == 0:
+                nc.scalar.copy(w1_bf[b][:].rearrange("p (c j) i -> p c i j", j=4),
+                               w1_raw[b][:].rearrange("p i (c j) -> p c i j", j=4))
+            else:
+                nc.gpsimd.tensor_scalar(w1_bf[b][:], w1_raw[b][:].rearrange("p i c -> p c i"), 1.0, 0.0,
+                                        ALU.mult, ALU.add)
 
         def quantize(words, scales, values):
             nc.vector.quantize_mx(out=words[:].bitcast(E4M3), scales=scales[:],
@@ -128,9 +141,12 @@ def tile_list_cellar_bottle_scores_kernel(
         nc.vector.tensor_copy(v_s[:], tab_s[:].indirect(idx[:]))
         quantize(w1_w[0], w1_s[0], w1_bf[0])
 
-        turned = psum.tile([P, PACK, P], F32, name="turned", tag="turned", bufs=3)
-        nc.tensor.transpose(turned[:, 0, :], rows[:], ident[:])
-        nc.scalar.copy(cols[:], turned[:, 0, 0:2 * TILES])
+        def to_columns(k):
+            tb = psum.tile([P, PACK, P], F32, name="turned", tag="turned", bufs=3)
+            nc.tensor.transpose(tb[:, 0, :], rows[k][:], ident[:])
+            nc.scalar.copy(cols[k][:], tb[:, 0, 0:TILES])
+
+        to_columns(0)
 
         for c0 in range(0, S, 256):
             gather_words(v_w[1], tab_w[1], idx, c0, c0 + 256)
@@ -143,12 +159,12 @@ def tile_list_cellar_bottle_scores_kernel(
             nc.tensor.matmul_mx(out=f[:], lhsT=v_w[1][:, jc].bitcast(E4M3), lhsT_scale=v_s[:, jc],
                                 rhs=w4_w[:, 2 * b * BANK:2 * (b + 1) * BANK].bitcast(E2M1),
                                 rhs_scale=w4_s[:, b * BANK:(b + 1) * BANK], start=False, stop=True)
-            if u < 3:
-                th = placed([P, PACK, P], F32, "th%d" % u, T + u * T // 2)
+            if u == 2:
+                th = placed([P, PACK, P], F32, "th2", 2 * T)
             else:
                 th = ring.tile([P, PACK, P], F32, name="th", tag="th", bufs=6)
             nc.scalar.activation(th[:], f[:].rearrange("p (q i) -> p i q", i=PACK), ACT.Tanh,
-                                 scale=cols[:, jt:jt + 1])
+                                 scale=cols[0][:, jt:jt + 1])
             return th
 
         def turn_on_vector(b, jt, th):
@@ -214,34 +230,35 @@ def tile_list_cellar_bottle_scores_kernel(
             if u >= 10:
                 scores(u - 10, 0)
 
+        to_columns(1)
         looked, picked, weighed = {}, {}, {}
 
         def look(t):
             nc.scalar.mul(neg_top[t][:], top[t][:], -1.0)
-            looked[t] = ring.tile([P, NP], F32, name="looked")
+            looked[t] = ring.tile([P, NP], F32, name="looked", bufs=2)
             nc.scalar.activation(looked[t][:], e_sb[t][:].indirect(p1[:]), ACT.Exp, bias=neg_top[t][:])
 
         def pick(t):
-            picked[t] = ring.tile([P, NP], F32, name="picked")
+            picked[t] = ring.tile([P, NP], F32, name="picked", bufs=2)
             nc.vector.tensor_copy(picked[t][:], e_sb[t][:].indirect(p2[:]))
 
         def weigh(t):
-            weighed[t] = ring.tile([P, NP], F32, name="weighed")
-            nc.vector.tensor_tensor(weighed[t][:], looked[t][:], mood_sb[t // 4][:, t % 4, :], ALU.mult)
+            weighed[t] = ring.tile([P, NP], F32, name="weighed", bufs=2)
+            nc.gpsimd.tensor_tensor(weighed[t][:], looked[t][:], mood_sb[t // 4][:, t % 4, :], ALU.mult)
 
         def finish(t):
             res = ring.tile([P, NP], F32, name="res")
-            nc.vector.scalar_tensor_tensor(res[:], picked[t][:], cols[:, TILES + t:TILES + t + 1],
+            nc.vector.scalar_tensor_tensor(res[:], picked[t][:], cols[1][:, t:t + 1],
                                            weighed[t][:], ALU.mult, ALU.max)
             nc.sync.dma_start(out[t * P:(t + 1) * P, :], res[:])
 
-        for t in range(TILES + 1):
+        for t in range(TILES + 2):
             if t < TILES:
                 scores(t, 1)
                 look(t)
-            if t > 0:
-                weigh(t - 1)
+            if 1 <= t <= TILES:
+                pick(t - 1)
+            if t >= 2:
+                finish(t - 2)
             if t < TILES:
-                pick(t)
-            if t > 0:
-                finish(t - 1)
+                weigh(t)

@@ -21,7 +21,7 @@ P = 128
 PACK = 4
 BANK = 512
 TILES = S // P
-ON_SCALAR = (3, 4, 5, 6)
+ON_SCALAR = (2, 4, 6)
 
 
 def tile_list_cellar_bottle_scores_kernel(
@@ -48,8 +48,8 @@ def tile_list_cellar_bottle_scores_kernel(
         idx2 = held([P, S2 // 16], U16, "idx2")
         p1 = held([P, NP // 16], U16, "p1")
         p2 = held([P, NP // 16], U16, "p2")
-        tab_w = [placed([P, T], I32, "tab_w0", 8 * T), held([P, T], I32, "tab_w1")]
-        tab_s = placed([P, T], U8, "tab_s", 0)
+        tab_w = [held([P, T], I32, "tab_w%d" % a) for a in range(2)]
+        tab_s = held([P, T], U8, "tab_s")
         tab2_w = [held([P, T3], I32, "tab2_w%d" % a) for a in range(2)]
         tab2_s = held([P, T3], U8, "tab2_s")
         w1_raw = [held([P, PACK, BANK], F32, "w1_raw%d" % b) for b in range(2)]
@@ -61,43 +61,64 @@ def tile_list_cellar_bottle_scores_kernel(
         ident = held([P, P], F32, "ident")
         mood_sb = [held([P, TILES // 2, NP], F32, "mood%d" % g) for g in range(2)]
 
-        nc.gpsimd.memset(tab_s[:].bitcast(I32), 0)
-        nc.vector.memset(w4_s[:].bitcast(I32), 0)
-        nc.vector.memset(tab2_s[:].bitcast(I32), 0)
+        v_w = [held([P, S], U32, "v_w%d" % a) for a in range(2)]
+        v_rows = held([P, S], U8, "v_rows")
+        v_s = held([P, S], U8, "v_s")
+        v2_w = [[placed([P, BANK], U32, "v2_w00", 0), placed([P, BANK], U32, "v2_w01", 2 * T)],
+                [placed([P, BANK], U32, "v2_w10", 4 * T), placed([P, BANK], U32, "v2_w11", 2 * T + T // 2)]]
+        v2_rows = held([P, S2], U8, "v2_rows")
+        v2_s = held([P, S2], U8, "v2_s")
+
+        for tile in (tab_s, tab2_s):
+            nc.vector.memset(tile[0:96, :].bitcast(I32), 0)
+        for tile in (v_s, w4_s, v2_s):
+            nc.gpsimd.memset(tile[:].bitcast(I32), 0)
         for tile in rows:
-            nc.vector.memset(tile[:], 0.0)
+            nc.gpsimd.memset(tile[:], 0.0)
         make_identity(nc, ident[:])
 
-        def load_words(tile, dram, pieces):
-            width = tile.shape[1] // pieces
-            for c0 in range(0, tile.shape[1], width):
-                nc.sync.dma_start(tile[:, c0:c0 + width], words_of(dram)[:, c0:c0 + width])
+        def load_words(a, half):
+            cs = slice(half * T // 2, (half + 1) * T // 2)
+            nc.sync.dma_start(tab_w[a][:, cs], words_of(tab_words[a])[:, cs])
 
-        def load_tab_scales(n):
-            a, r = divmod(n, 4)
-            nc.sync.dma_start(tab_s[4 * (1 - a) + r:P:32, :].bitcast(I32), tab_scales[a, r:16:4, :].bitcast(I32))
+        def load_scale_rows(tile, dram):
+            nc.sync.dma_start(tile[96:P, :].bitcast(I32), dram.rearrange("a q t -> (a q) t").bitcast(I32))
+
+        def spread(plane, picked_rows, a, q, first):
+            nc.sync.dma_start(plane[32 * q + first:32 * q + first + 4, :].bitcast(I32),
+                              picked_rows[96 + 16 * a + 4 * q:96 + 16 * a + 4 * q + 4, :].bitcast(I32))
+
+        def spread_tab(n):
+            a, q = divmod(n, 4)
+            spread(v_s, v_rows, a, q, 4 * (1 - a))
 
         w1_rows = w1.rearrange("(p i) r -> p i r", i=PACK)
-        load_words(tab_w[0], tab_words[0], 2)
+        load_scale_rows(tab_s, tab_scales)
         nc.sync.dma_start(idx[:], offs)
-        for n in range(5):
-            load_tab_scales(n)
+        load_scale_rows(tab2_s, tab2_scales)
+        nc.sync.dma_start(idx2[:], offs2)
+        load_words(0, 0)
+        load_words(0, 1)
         nc.sync.dma_start(w1_raw[0][:], w1_rows[:, :, 0:BANK])
-        for n in range(5, 8):
-            load_tab_scales(n)
-        load_words(tab_w[1], tab_words[1], 2)
         nc.sync.dma_start(w4_w[:].bitcast(I32), w4_words[0].bitcast(I32))
+        nc.vector.tensor_copy(v_rows[:], tab_s[:].indirect(idx[:]))
+        nc.vector.tensor_copy(v2_rows[:], tab2_s[:].indirect(idx2[:]))
+        for n in range(4):
+            spread_tab(n)
+        load_words(1, 0)
+        for n in range(4, 8):
+            spread_tab(n)
+        load_words(1, 1)
+        nc.sync.dma_start(rows[0][0:TILES, :], place.rearrange("(t p) -> t p", p=P))
         for r in range(4):
             nc.sync.dma_start(w4_s[r:P:32, :].bitcast(I32), w4_scales[0, r:16:4, :].bitcast(I32))
-        nc.sync.dma_start(rows[0][0:TILES, :], place.rearrange("(t p) -> t p", p=P))
-        nc.sync.dma_start(w1_raw[1][:], w1_rows[:, :, BANK:H])
         nc.sync.dma_start(gain_sb[:], gain.rearrange("(b p i) -> p b i", b=2, i=PACK))
-        nc.sync.dma_start(idx2[:], offs2)
-        for q in range(4):
-            nc.sync.dma_start(tab2_s[32 * q:32 * q + 8, :].bitcast(I32),
-                              tab2_scales[:, 4 * q:4 * q + 4, :].bitcast(I32))
+        nc.sync.dma_start(w1_raw[1][:], w1_rows[:, :, BANK:H])
         for a in range(2):
-            load_words(tab2_w[a], tab2_words[a], 1)
+            nc.sync.dma_start(tab2_w[a][:], words_of(tab2_words[a]))
+        for a in range(2):
+            for q in range(4):
+                spread(v2_s, v2_rows, a, q, 4 * a)
         nc.sync.dma_start(rows[1][0:TILES, :], cust.rearrange("(t p) -> t p", p=P))
         nc.sync.dma_start(p1[:], pos1)
         nc.sync.dma_start(p2[:], pos2)
@@ -105,14 +126,10 @@ def tile_list_cellar_bottle_scores_kernel(
         for g in range(2):
             nc.sync.dma_start(mood_sb[g][:], mood_rows[:, g * 4:(g + 1) * 4, :])
 
-        v_w = [held([P, S], U32, "v_w0"), placed([P, S], U32, "v_w1", 0)]
-        v_s = placed([P, S], U8, "v_s", 8 * T)
-        v2_w = [placed([P, S2], U32, "v2_w0", 3 * T), placed([P, S2], U32, "v2_w1", 7 * T)]
-        v2_s = placed([P, S2], U8, "v2_s", 2 * T)
-        w1_bf = [held([P, BANK, PACK], BF16, "w1_bf0"), placed([P, BANK, PACK], BF16, "w1_bf1", 7 * T)]
+        w1_bf = [held([P, BANK, PACK], BF16, "w1_bf0"), placed([P, BANK, PACK], BF16, "w1_bf1", 4 * T)]
         w1_w = [held([P, BANK], U32, "w1_w%d" % b) for b in range(2)]
         w1_s = [held([P, BANK], U8, "w1_s%d" % b) for b in range(2)]
-        h_bf = [[placed([P, BANK, PACK], BF16, "h_bf%d%d" % (b, g), (3 + 2 * b + g) * T) for g in range(2)]
+        h_bf = [[placed([P, BANK, PACK], BF16, "h_bf%d%d" % (b, g), (2 * b + g) * T) for g in range(2)]
                 for b in range(2)]
         h_w = [[held([P, BANK], U32, "h_w%d%d" % (b, g)) for g in range(2)] for b in range(2)]
         h_s = [[held([P, BANK], U8, "h_s%d%d" % (b, g)) for g in range(2)] for b in range(2)]
@@ -121,24 +138,24 @@ def tile_list_cellar_bottle_scores_kernel(
         top = [held([P, 1], F32, "top%d" % t) for t in range(TILES)]
         neg_top = [held([P, 1], F32, "neg_top%d" % t) for t in range(TILES)]
 
-        def gather_words(dst, table, lst, c0, c1):
-            nc.vector.tensor_copy(dst[:, c0:c1], table[:].bitcast(U32).indirect(lst[:, c0 // 16:c1 // 16]))
+        def gather_words(dst, table, lst, c0):
+            entries = dst.shape[1]
+            nc.vector.tensor_copy(dst, table[:].bitcast(U32).indirect(lst[:, c0 // 16:(c0 + entries) // 16]))
 
-        def round_w1(b):
-            if b == 0:
-                nc.scalar.copy(w1_bf[b][:].rearrange("p (c j) i -> p c i j", j=4),
-                               w1_raw[b][:].rearrange("p i (c j) -> p c i j", j=4))
-            else:
-                nc.gpsimd.tensor_scalar(w1_bf[b][:], w1_raw[b][:].rearrange("p i c -> p c i"), 1.0, 0.0,
-                                        ALU.mult, ALU.add)
+        def round_w1_on_scalar(b, cs):
+            nc.scalar.copy(w1_bf[b][:, cs, :].rearrange("p (c j) i -> p c i j", j=4),
+                           w1_raw[b][:, :, cs].rearrange("p i (c j) -> p c i j", j=4))
+
+        def round_w1_on_gpsimd(b, cs):
+            nc.gpsimd.tensor_scalar(w1_bf[b][:, cs, :], w1_raw[b][:, :, cs].rearrange("p i c -> p c i"), 1.0, 0.0,
+                                    ALU.mult, ALU.add)
 
         def quantize(words, scales, values):
             nc.vector.quantize_mx(out=words[:].bitcast(E4M3), scales=scales[:],
                                   in_=values[:].rearrange("p c i -> p (c i)"))
 
-        gather_words(v_w[0], tab_w[0], idx, 0, S)
-        round_w1(0)
-        nc.vector.tensor_copy(v_s[:], tab_s[:].indirect(idx[:]))
+        gather_words(v_w[0][:], tab_w[0], idx, 0)
+        round_w1_on_scalar(0, slice(0, BANK))
         quantize(w1_w[0], w1_s[0], w1_bf[0])
 
         def to_columns(k):
@@ -149,9 +166,9 @@ def tile_list_cellar_bottle_scores_kernel(
         to_columns(0)
 
         for c0 in range(0, S, 256):
-            gather_words(v_w[1], tab_w[1], idx, c0, c0 + 256)
+            gather_words(v_w[1][:, c0:c0 + 256], tab_w[1], idx, c0)
 
-        def features(u, b, jt):
+        def features(b, jt):
             jc = slice(jt * P, (jt + 1) * P)
             f = psum.tile([P, BANK], F32, name="f", tag="f", bufs=3)
             nc.tensor.matmul_mx(out=f[:], lhsT=v_w[0][:, jc].bitcast(E4M3), lhsT_scale=v_s[4:P, jc],
@@ -159,10 +176,7 @@ def tile_list_cellar_bottle_scores_kernel(
             nc.tensor.matmul_mx(out=f[:], lhsT=v_w[1][:, jc].bitcast(E4M3), lhsT_scale=v_s[:, jc],
                                 rhs=w4_w[:, 2 * b * BANK:2 * (b + 1) * BANK].bitcast(E2M1),
                                 rhs_scale=w4_s[:, b * BANK:(b + 1) * BANK], start=False, stop=True)
-            if u == 2:
-                th = placed([P, PACK, P], F32, "th2", 2 * T)
-            else:
-                th = ring.tile([P, PACK, P], F32, name="th", tag="th", bufs=6)
+            th = ring.tile([P, PACK, P], F32, name="th", tag="th", bufs=6)
             nc.scalar.activation(th[:], f[:].rearrange("p (q i) -> p i q", i=PACK), ACT.Tanh,
                                  scale=cols[0][:, jt:jt + 1])
             return th
@@ -205,7 +219,7 @@ def tile_list_cellar_bottle_scores_kernel(
             mc = slice(t * P, (t + 1) * P)
             acc = psum.tile([P, BANK], F32, name="acc", tag="acc", bufs=2)
             for b in range(2):
-                nc.tensor.matmul_mx(out=acc[:], lhsT=v2_w[b][:, mc].bitcast(E4M3), lhsT_scale=v2_s[4 * b:P, mc],
+                nc.tensor.matmul_mx(out=acc[:], lhsT=v2_w[b][t // 4][:, (t % 4) * P:(t % 4 + 1) * P].bitcast(E4M3), lhsT_scale=v2_s[4 * b:P, mc],
                                     rhs=h_w[b][g][:].bitcast(E4M3), rhs_scale=h_s[b][g][:],
                                     start=(b == 0), stop=(b == 1))
             nc.vector.tensor_scalar(e_sb[t][:, g * BANK:(g + 1) * BANK], acc[:], 1.0,
@@ -216,17 +230,16 @@ def tile_list_cellar_bottle_scores_kernel(
         tanhs = []
         for u in range(len(units) + 2):
             if u < len(units):
-                tanhs.append(features(u, *units[u]))
+                tanhs.append(features(*units[u]))
             if u >= 2:
                 turn(u - 2)
             if u == 3:
-                round_w1(1)
+                round_w1_on_gpsimd(1, slice(0, BANK // 2))
+                round_w1_on_scalar(1, slice(BANK // 2, BANK))
                 quantize(w1_w[1], w1_s[1], w1_bf[1])
-            if u == 4:
-                nc.vector.tensor_copy(v2_s[:], tab2_s[:].indirect(idx2[:]))
-            if u in (5, 6, 7, 8):
-                a, half = divmod(u - 5, 2)
-                gather_words(v2_w[a], tab2_w[a], idx2, half * BANK, (half + 1) * BANK)
+            if u in (5, 6, 10, 11):
+                half, a = divmod(u, 5)
+                gather_words(v2_w[a][half - 1][:], tab2_w[a], idx2, (half - 1) * BANK)
             if u >= 10:
                 scores(u - 10, 0)
 

@@ -228,20 +228,25 @@ def tile_list_cellar_bottle_scores_kernel(
 
         units = [(b, jt) for g in range(2) for b in range(2) for jt in range(4 * g, 4 * g + 4)]
         tanhs = []
-        for u in range(len(units) + 2):
-            if u < len(units):
-                tanhs.append(features(*units[u]))
+        for u in range(0, len(units) + 2, 2):
+            for unit in units[u:u + 2]:
+                tanhs.append(features(*unit))
+            if u >= 10:
+                scores(u - 10, 0)
+                scores(u - 9, 0)
             if u >= 2:
                 turn(u - 2)
-            if u == 3:
+                turn(u - 1)
+            if u == 2:
                 round_w1_on_gpsimd(1, slice(0, BANK // 2))
                 round_w1_on_scalar(1, slice(BANK // 2, BANK))
                 quantize(w1_w[1], w1_s[1], w1_bf[1])
-            if u in (5, 6, 10, 11):
-                half, a = divmod(u, 5)
-                gather_words(v2_w[a][half - 1][:], tab2_w[a], idx2, (half - 1) * BANK)
-            if u >= 10:
-                scores(u - 10, 0)
+            if u in (4, 6):
+                a = (u - 4) // 2
+                gather_words(v2_w[a][0][:], tab2_w[a], idx2, 0)
+            if u == 10:
+                for a in range(2):
+                    gather_words(v2_w[a][1][:], tab2_w[a], idx2, BANK)
 
         to_columns(1)
         looked, picked, weighed = {}, {}, {}

from contextlib import ExitStack

import concourse.mybir as mybir
from concourse.masks import make_identity

K, K1, H, T, S, S2, T3, NP = 1024, 512, 1024, 4096, 1024, 1024, 2048, 512
FLOPS = 2 * K * H * S + 2 * H * S * S2

F32 = mybir.dt.float32
BF16 = mybir.dt.bfloat16
I32 = mybir.dt.int32
U32 = mybir.dt.uint32
U16 = mybir.dt.uint16
U8 = mybir.dt.uint8
E4M3 = mybir.dt.float8_e4m3fn_x4
E2M1 = mybir.dt.float4_e2m1fn_x4
ACT = mybir.ActivationFunctionType
ALU = mybir.AluOpType

P = 128
PACK = 4
BANK = 512
TILES = S // P
ON_SCALAR = (2, 4, 6)


def tile_list_cellar_bottle_scores_kernel(
    tc, tab_words, tab_scales, offs, tab2_words, tab2_scales, offs2, pos1, pos2,
    w1, w4_words, w4_scales, place, gain, mood, cust, out,
):
    nc = tc.nc
    with ExitStack() as ctx:
        keep = ctx.enter_context(tc.tile_pool(name="keep", bufs=1))
        ring = ctx.enter_context(tc.tile_pool(name="ring", bufs=3))
        shared = ctx.enter_context(tc.tile_pool(name="shared", bufs=1))
        psum = ctx.enter_context(tc.psum_pool(name="psum", bufs=1))

        def held(shape, dtype, name):
            return keep.tile(shape, dtype, name=name, align_bytes=64)

        def placed(shape, dtype, name, offset):
            return shared.tile(shape, dtype, name=name, align_bytes=64, offset=offset)

        def words_of(dram):
            return dram.rearrange("p t i -> p (t i)").bitcast(I32)

        idx = held([P, S // 16], U16, "idx")
        idx2 = held([P, S2 // 16], U16, "idx2")
        p1 = held([P, NP // 16], U16, "p1")
        p2 = held([P, NP // 16], U16, "p2")
        tab_w = [held([P, T], I32, "tab_w%d" % a) for a in range(2)]
        tab_s = held([P, T], U8, "tab_s")
        tab2_w = [held([P, T3], I32, "tab2_w%d" % a) for a in range(2)]
        tab2_s = held([P, T3], U8, "tab2_s")
        w1_raw = [held([P, PACK, BANK], F32, "w1_raw%d" % b) for b in range(2)]
        w4_w = held([P, 2 * H], U8, "w4_w")
        w4_s = held([P, H], U8, "w4_s")
        gain_sb = held([P, 2, PACK], F32, "gain_sb")
        rows = [held([P, P], F32, "rows%d" % k) for k in range(2)]
        cols = [held([P, TILES], F32, "cols%d" % k) for k in range(2)]
        ident = held([P, P], F32, "ident")
        mood_sb = [held([P, TILES // 2, NP], F32, "mood%d" % g) for g in range(2)]

        v_w = [held([P, S], U32, "v_w%d" % a) for a in range(2)]
        v_rows = held([P, S], U8, "v_rows")
        v_s = held([P, S], U8, "v_s")
        v2_w = [[placed([P, BANK], U32, "v2_w00", 0), placed([P, BANK], U32, "v2_w01", 2 * T)],
                [placed([P, BANK], U32, "v2_w10", 4 * T), placed([P, BANK], U32, "v2_w11", 2 * T + T // 2)]]
        v2_rows = held([P, S2], U8, "v2_rows")
        v2_s = held([P, S2], U8, "v2_s")

        for tile in (tab_s, tab2_s):
            nc.vector.memset(tile[0:96, :].bitcast(I32), 0)
        for tile in (v_s, w4_s, v2_s):
            nc.gpsimd.memset(tile[:].bitcast(I32), 0)
        for tile in rows:
            nc.gpsimd.memset(tile[:], 0.0)
        make_identity(nc, ident[:])

        def load_words(a, half):
            cs = slice(half * T // 2, (half + 1) * T // 2)
            nc.sync.dma_start(tab_w[a][:, cs], words_of(tab_words[a])[:, cs])

        def load_scale_rows(tile, dram):
            nc.sync.dma_start(tile[96:P, :].bitcast(I32), dram.rearrange("a q t -> (a q) t").bitcast(I32))

        def spread(plane, picked_rows, a, q, first):
            nc.sync.dma_start(plane[32 * q + first:32 * q + first + 4, :].bitcast(I32),
                              picked_rows[96 + 16 * a + 4 * q:96 + 16 * a + 4 * q + 4, :].bitcast(I32))

        def spread_tab(n):
            a, q = divmod(n, 4)
            spread(v_s, v_rows, a, q, 4 * (1 - a))

        w1_rows = w1.rearrange("(p i) r -> p i r", i=PACK)
        load_scale_rows(tab_s, tab_scales)
        nc.sync.dma_start(idx[:], offs)
        load_scale_rows(tab2_s, tab2_scales)
        nc.sync.dma_start(idx2[:], offs2)
        load_words(0, 0)
        load_words(0, 1)
        nc.sync.dma_start(w1_raw[0][:], w1_rows[:, :, 0:BANK])
        nc.sync.dma_start(w4_w[:].bitcast(I32), w4_words[0].bitcast(I32))
        nc.vector.tensor_copy(v_rows[:], tab_s[:].indirect(idx[:]))
        nc.vector.tensor_copy(v2_rows[:], tab2_s[:].indirect(idx2[:]))
        for n in range(4):
            spread_tab(n)
        load_words(1, 0)
        for n in range(4, 8):
            spread_tab(n)
        load_words(1, 1)
        nc.sync.dma_start(rows[0][0:TILES, :], place.rearrange("(t p) -> t p", p=P))
        for r in range(4):
            nc.sync.dma_start(w4_s[r:P:32, :].bitcast(I32), w4_scales[0, r:16:4, :].bitcast(I32))
        nc.sync.dma_start(gain_sb[:], gain.rearrange("(b p i) -> p b i", b=2, i=PACK))
        nc.sync.dma_start(w1_raw[1][:], w1_rows[:, :, BANK:H])
        for a in range(2):
            nc.sync.dma_start(tab2_w[a][:], words_of(tab2_words[a]))
        for a in range(2):
            for q in range(4):
                spread(v2_s, v2_rows, a, q, 4 * a)
        nc.sync.dma_start(rows[1][0:TILES, :], cust.rearrange("(t p) -> t p", p=P))
        nc.sync.dma_start(p1[:], pos1)
        nc.sync.dma_start(p2[:], pos2)
        mood_rows = mood.rearrange("(t p) n -> p t n", p=P)
        for g in range(2):
            nc.sync.dma_start(mood_sb[g][:], mood_rows[:, g * 4:(g + 1) * 4, :])

        w1_bf = [held([P, BANK, PACK], BF16, "w1_bf0"), placed([P, BANK, PACK], BF16, "w1_bf1", 4 * T)]
        w1_w = [held([P, BANK], U32, "w1_w%d" % b) for b in range(2)]
        w1_s = [held([P, BANK], U8, "w1_s%d" % b) for b in range(2)]
        h_bf = [[placed([P, BANK, PACK], BF16, "h_bf%d%d" % (b, g), (2 * b + g) * T) for g in range(2)]
                for b in range(2)]
        h_w = [[held([P, BANK], U32, "h_w%d%d" % (b, g)) for g in range(2)] for b in range(2)]
        h_s = [[held([P, BANK], U8, "h_s%d%d" % (b, g)) for g in range(2)] for b in range(2)]
        e_sb = [held([P, S], F32, "e%d" % t) for t in range(TILES)]
        half_top = [held([P, 1], F32, "half_top%d" % t) for t in range(TILES)]
        top = [held([P, 1], F32, "top%d" % t) for t in range(TILES)]
        neg_top = [held([P, 1], F32, "neg_top%d" % t) for t in range(TILES)]

        def gather_words(dst, table, lst, c0):
            entries = dst.shape[1]
            nc.vector.tensor_copy(dst, table[:].bitcast(U32).indirect(lst[:, c0 // 16:(c0 + entries) // 16]))

        def round_w1_on_scalar(b, cs):
            nc.scalar.copy(w1_bf[b][:, cs, :].rearrange("p (c j) i -> p c i j", j=4),
                           w1_raw[b][:, :, cs].rearrange("p i (c j) -> p c i j", j=4))

        def round_w1_on_gpsimd(b, cs):
            nc.gpsimd.tensor_scalar(w1_bf[b][:, cs, :], w1_raw[b][:, :, cs].rearrange("p i c -> p c i"), 1.0, 0.0,
                                    ALU.mult, ALU.add)

        def quantize(words, scales, values):
            nc.vector.quantize_mx(out=words[:].bitcast(E4M3), scales=scales[:],
                                  in_=values[:].rearrange("p c i -> p (c i)"))

        gather_words(v_w[0][:], tab_w[0], idx, 0)
        round_w1_on_scalar(0, slice(0, BANK))
        quantize(w1_w[0], w1_s[0], w1_bf[0])

        def to_columns(k):
            tb = psum.tile([P, PACK, P], F32, name="turned", tag="turned", bufs=3)
            nc.tensor.transpose(tb[:, 0, :], rows[k][:], ident[:])
            nc.scalar.copy(cols[k][:], tb[:, 0, 0:TILES])

        to_columns(0)

        for c0 in range(0, S, 256):
            gather_words(v_w[1][:, c0:c0 + 256], tab_w[1], idx, c0)

        def features(b, jt):
            jc = slice(jt * P, (jt + 1) * P)
            f = psum.tile([P, BANK], F32, name="f", tag="f", bufs=3)
            nc.tensor.matmul_mx(out=f[:], lhsT=v_w[0][:, jc].bitcast(E4M3), lhsT_scale=v_s[4:P, jc],
                                rhs=w1_w[b][:].bitcast(E4M3), rhs_scale=w1_s[b][:], start=True, stop=False)
            nc.tensor.matmul_mx(out=f[:], lhsT=v_w[1][:, jc].bitcast(E4M3), lhsT_scale=v_s[:, jc],
                                rhs=w4_w[:, 2 * b * BANK:2 * (b + 1) * BANK].bitcast(E2M1),
                                rhs_scale=w4_s[:, b * BANK:(b + 1) * BANK], start=False, stop=True)
            th = ring.tile([P, PACK, P], F32, name="th", tag="th", bufs=6)
            nc.scalar.activation(th[:], f[:].rearrange("p (q i) -> p i q", i=PACK), ACT.Tanh,
                                 scale=cols[0][:, jt:jt + 1])
            return th

        def turn_on_vector(b, jt, th):
            tb = psum.tile([P, PACK, P], F32, name="turned", tag="turned", bufs=3)
            for i in range(PACK):
                nc.tensor.transpose(tb[:, i, :], th[:, i, :], ident[:])
            j0 = (jt % 4) * P
            nc.vector.tensor_tensor(h_bf[b][jt // 4][:, j0:j0 + P, :], tb[:].rearrange("p i j -> p j i"),
                                    gain_sb[:, b:b + 1, :].to_broadcast([P, P, PACK]), ALU.mult)

        def turn_on_scalar(b, i0, pair, planes):
            tb = psum.tile([P, 2, 2 * P], F32, name="turned", tag="turned", bufs=3)
            for i in range(i0, i0 + 2):
                for k, th in enumerate(pair):
                    nc.tensor.transpose(tb[:, i - i0, k * P:(k + 1) * P], th[:, i, :], ident[:])
            for i in range(i0, i0 + 2):
                nc.scalar.activation(planes[:, i, :], tb[:, i - i0, :], ACT.Copy, scale=gain_sb[:, b, i:i + 1])

        planes_of = {}

        def turn(u):
            b, jt = units[u]
            n, second = divmod(u, 2)
            if n in ON_SCALAR:
                if not second:
                    planes_of[n] = ring.tile([P, PACK, 2 * P], BF16, name="planes", bufs=2)
                turn_on_scalar(b, 2 * second, tanhs[2 * n:2 * n + 2], planes_of[n])
                if second:
                    j0 = ((jt - 1) % 4) * P
                    nc.scalar.copy(h_bf[b][jt // 4][:, j0:j0 + 2 * P, :].rearrange("p (c j) i -> p c i j", j=4),
                                   planes_of[n][:].rearrange("p i (c j) -> p c i j", j=4))
            else:
                turn_on_vector(b, jt, tanhs[u])
            if jt % 4 == 3:
                quantize(h_w[b][jt // 4], h_s[b][jt // 4], h_bf[b][jt // 4])

        def scores(t, g):
            mc = slice(t * P, (t + 1) * P)
            acc = psum.tile([P, BANK], F32, name="acc", tag="acc", bufs=2)
            for b in range(2):
                nc.tensor.matmul_mx(out=acc[:], lhsT=v2_w[b][t // 4][:, (t % 4) * P:(t % 4 + 1) * P].bitcast(E4M3), lhsT_scale=v2_s[4 * b:P, mc],
                                    rhs=h_w[b][g][:].bitcast(E4M3), rhs_scale=h_s[b][g][:],
                                    start=(b == 0), stop=(b == 1))
            nc.vector.tensor_scalar(e_sb[t][:, g * BANK:(g + 1) * BANK], acc[:], 1.0,
                                    half_top[t][:] if g == 1 else None, ALU.mult, ALU.max,
                                    accum_out=(top if g == 1 else half_top)[t][:])

        units = [(b, jt) for g in range(2) for b in range(2) for jt in range(4 * g, 4 * g + 4)]
        tanhs = []
        for u in range(0, len(units) + 2, 2):
            for unit in units[u:u + 2]:
                tanhs.append(features(*unit))
            if u >= 10:
                scores(u - 10, 0)
                scores(u - 9, 0)
            if u >= 2:
                turn(u - 2)
                turn(u - 1)
            if u == 2:
                round_w1_on_gpsimd(1, slice(0, BANK // 2))
                round_w1_on_scalar(1, slice(BANK // 2, BANK))
                quantize(w1_w[1], w1_s[1], w1_bf[1])
            if u in (4, 6):
                a = (u - 4) // 2
                gather_words(v2_w[a][0][:], tab2_w[a], idx2, 0)
            if u == 10:
                for a in range(2):
                    gather_words(v2_w[a][1][:], tab2_w[a], idx2, BANK)

        to_columns(1)
        looked, picked, weighed = {}, {}, {}

        def look(t):
            nc.scalar.mul(neg_top[t][:], top[t][:], -1.0)
            looked[t] = ring.tile([P, NP], F32, name="looked", bufs=2)
            nc.scalar.activation(looked[t][:], e_sb[t][:].indirect(p1[:]), ACT.Exp, bias=neg_top[t][:])

        def pick(t):
            picked[t] = ring.tile([P, NP], F32, name="picked", bufs=2)
            nc.vector.tensor_copy(picked[t][:], e_sb[t][:].indirect(p2[:]))

        def weigh(t):
            weighed[t] = ring.tile([P, NP], F32, name="weighed", bufs=2)
            nc.gpsimd.tensor_tensor(weighed[t][:], looked[t][:], mood_sb[t // 4][:, t % 4, :], ALU.mult)

        def finish(t):
            res = ring.tile([P, NP], F32, name="res")
            nc.vector.scalar_tensor_tensor(res[:], picked[t][:], cols[1][:, t:t + 1],
                                           weighed[t][:], ALU.mult, ALU.max)
            nc.sync.dma_start(out[t * P:(t + 1) * P, :], res[:])

        for t in range(TILES + 2):
            if t < TILES:
                scores(t, 1)
                look(t)
            if 1 <= t <= TILES:
                pick(t - 1)
            if t >= 2:
                finish(t - 2)
            if t < TILES:
                weigh(t)
